import numpy as np, ml_dtypes
CORES = [23,119,17,113]
N = 4
NB, B = 12, 32
def setup_inputs(rng):
    return {"x": rng.standard_normal((N, 128, NB * B), dtype=np.float32).astype(ml_dtypes.bfloat16), "wv": (rng.standard_normal((N, 128, 128), dtype=np.float32) / 16).astype(ml_dtypes.bfloat16), "wh": (rng.standard_normal((N, 128, 128), dtype=np.float32) / 16).astype(ml_dtypes.bfloat16)}
def setup_inputs_big(rng):
    d = setup_inputs(rng)
    for k in ("x",): d[k] = (d[k].astype(np.float32) * 1048576.0).astype(d[k].dtype)
    return d
def setup_inputs_small(rng):
    d = setup_inputs(rng)
    for k in ("x",): d[k] = (d[k].astype(np.float32) * (1 / 1048576.0)).astype(d[k].dtype)
    return d
def setup_inputs_apart(rng):
    d = setup_inputs(rng)
    f = (10.0 ** rng.permutation(np.linspace(-1.5, 1.5, N))).astype(np.float32).reshape(N, 1, 1)
    for k in ("x",): d[k] = (d[k].astype(np.float32) * f).astype(d[k].dtype)
    return d
def reference(x, wv, wh):
    X, WV, WH = x.astype(np.float64), wv.astype(np.float64), wh.astype(np.float64)
    h = np.zeros((N, NB, 128, B))
    for r in range(N):
        for c in range(NB):
            a = X[r][:, B * c:B * c + B].copy()
            if r: a += WV[r].T @ h[r - 1][c]
            if c: a += WH[r].T @ h[r][c - 1]
            h[r][c] = np.maximum(a, 0.0)
    return {"y": np.concatenate([h[:, c] for c in range(NB)], axis=2).astype(ml_dtypes.bfloat16)}

@@ -1,0 +1,173 @@
+from concourse.bass import DstId, RemoteDMATransfer
+from concourse.mybir import AluOpType
+
+N, NB, B = 4, 12, 32
+XO = 256
+W = XO + NB * B
+J = [6, 4, 4, 6]
+STORES = [(0, 5), (5, 9), (9, 11), (11, 12)]
+NBANK = 8
+
+SCRATCH = {
+    "isrc": ("sbuf", [128, 129], "bfloat16"),
+    "idd": ("dram", [1, 128 * 129], "bfloat16"),
+    "ident": ("sbuf", [128, 128], "bfloat16"),
+    "zeros": ("sbuf", [128, B], "float32"),
+    "zb": ("sbuf", [128, B], "bfloat16"),
+}
+for _q in range(N):
+    SCRATCH["inb%d" % _q] = ("sbuf", [128, W], "bfloat16")
+    SCRATCH["h%d" % _q] = ("sbuf", [128, NB * B], "bfloat16")
+for _b in range(NBANK):
+    SCRATCH["ps%d" % _b] = ("psum", [128, 512], "float32")
+
+SEMAPHORES = ["ld1", "ld2", "ms", "idw", "idn", "mm", "vd", "st", "sent"] + [
+    "a%d_%d" % (q, p) for q in range(N - 1) for p in range(2)]
+
+
+def _count(m):
+    return bin(m).count("1")
+
+
+def _plan(q, cores, topo):
+    src = cores[q]
+    dests = list(range(N - 1, q, -1))
+    narrow = topo.mask(src, cores[dests[0]])
+    for d in dests:
+        narrow &= topo.mask(src, cores[d])
+    rounds = []
+    for d in dests:
+        m = topo.mask(src, cores[d])
+        if topo.chip(src) != topo.chip(cores[d]):
+            m = narrow
+        else:
+            m = (m & ~narrow) or m
+        for rd in rounds:
+            if all((m & mm) == 0 for _, mm in rd):
+                rd.append((d, m))
+                break
+        else:
+            rounds.append([(d, m)])
+    return rounds
+
+
+def rank_program(g, core, T, topo):
+    R = T.rank_of(core)
+    if R is None:
+        return
+    S = T.sem
+    cores = list(T.cores)
+    inb = [T["inb%d" % q] for q in range(N)]
+    H = [T["h%d" % q] for q in range(N)]
+    ps = [T["ps%d" % b] for b in range(NBANK)]
+    te, ve = g.tensor, g.vector
+    own = inb[R]
+    split = XO + B * J[R]
+
+    g.sync.dma_start(own[:, 128:256], T.wh[:, :]).then_inc(S.ld1, 16)
+    if R > 0:
+        g.scalar.dma_start(own[:, 0:128], T.wv[:, :]).then_inc(S.ld1, 16)
+        g.sync.dma_start(own[:, XO:split], T.x[:, 0:B * J[R]]).then_inc(S.ld1, 16)
+        LD1 = 48
+    else:
+        g.scalar.dma_start(own[:, XO:split], T.x[:, 0:B * J[R]]).then_inc(S.ld1, 16)
+        LD1 = 32
+    g.sync.dma_start(own[:, split:W], T.x[:, B * J[R]:NB * B]).then_inc(S.ld2, 16)
+
+    ve.memset(T.isrc[:, 0:1], 1.0).then_inc(S.ms, 1)
+    ve.memset(T.isrc[:, 1:129], 0.0).then_inc(S.ms, 1)
+    ve.memset(T.zeros[:, :], 0.0).then_inc(S.ms, 1)
+    ve.memset(T.zb[:, :], 0.0).then_inc(S.ms, 1)
+    ve.wait_ge(S.ms, 4)
+    g.scalar.wait_ge(S.ms, 4)
+    g.scalar.dma_start(T.idd[0, :], T.isrc[:, :]).then_inc(S.idw, 16)
+    g.scalar.wait_ge(S.idw, 16)
+    g.scalar.dma_start(T.ident[:, :], T.idd[0, 0:128 * 128]).then_inc(S.idn, 16)
+    ident = T.ident[:, :]
+
+    sent = 0
+    if R < N - 1:
+        lo = 0 if R > 0 else 128
+        pieces = [(lo, split), (split, W)]
+        rounds = _plan(R, cores, topo)
+        for p, (a, b) in enumerate(pieces):
+            g.wait_ge(S.ld1 if p == 0 else S.ld2, LD1 if p == 0 else 16)
+            for rd in rounds:
+                trs = []
+                for d, m in rd:
+                    assert topo.may_write(core, cores[d])
+                    rid, pid, _ = topo.addr(cores[d])
+                    trs.append(RemoteDMATransfer(dst_ids=[DstId(rid=rid, pnc=pid)], dma_engine_mask=m,
+                                                 remote_sem=S["a%d_%d" % (R, p)], src=own[:, a:b], dst=own[:, a:b]))
+                    sent += _count(m)
+                g.remote_dma_fused(trs, local_sem=S.sent)
+
+    arrive = {}
+    for q in range(R):
+        for rd in _plan(q, cores, topo):
+            for d, m in rd:
+                if d == R:
+                    arrive[q] = _count(m)
+
+    order = [(r, s - r) for s in range(NB + R) for r in range(R + 1) if 0 <= s - r < NB]
+    idx = {nd: i for i, nd in enumerate(order)}
+    mn = [nd for nd in order if nd != (0, 0)]
+    ahead = max(2, R + 1)
+    seen = set()
+    tw = [0]
+
+    def here(queue, tag, r, half):
+        if (tag, r, half) in seen:
+            return
+        seen.add((tag, r, half))
+        if r == R:
+            queue.wait_ge(S.ld1 if half == 0 else S.ld2, LD1 if half == 0 else 16)
+        else:
+            queue.wait_ge(S["a%d_%d" % (r, half)], arrive[r])
+
+    def done(n):
+        if n > tw[0]:
+            te.wait_ge(S.vd, n)
+            tw[0] = n
+
+    def preload(k):
+        r, c = mn[k]
+        here(te, "t", r, 0)
+        if c >= J[r]:
+            here(te, "t", r, 1)
+        if k >= NBANK:
+            done(idx[mn[k - NBANK]] + 1)
+        te.matmul(ps[k % NBANK][:, 0:B], ident, inb[r][:, XO + B * c:XO + B * c + B], True, False)
+
+    te.wait_ge(S.idn, 16)
+    here(ve, "v", 0, 0)
+    ve.tensor_tensor(H[0][:, 0:B], inb[0][:, XO:XO + B], T.zb[:, :], AluOpType.max).then_inc(S.vd, 1)
+    for k in range(min(ahead, len(mn))):
+        preload(k)
+    for k, (r, c) in enumerate(mn):
+        if k + ahead < len(mn):
+            preload(k + ahead)
+        acc = ps[k % NBANK][:, 0:B]
+        mms = []
+        need = 0
+        if r > 0:
+            mms.append((inb[r][:, 0:128], H[r - 1][:, B * c:B * c + B]))
+            need = max(need, idx[(r - 1, c)] + 1)
+        if c > 0:
+            mms.append((inb[r][:, 128:256], H[r][:, B * (c - 1):B * c]))
+            need = max(need, idx[(r, c - 1)] + 1)
+        done(need)
+        for i, (w, h) in enumerate(mms):
+            ins = te.matmul(acc, w, h, False, i == len(mms) - 1)
+        ins.then_inc(S.mm, 1)
+        ve.wait_ge(S.mm, k + 1)
+        ve.tensor_tensor(H[r][:, B * c:B * c + B], acc, T.zeros[:, :], AluOpType.max).then_inc(S.vd, 1)
+
+    for i, (a, b) in enumerate(STORES):
+        q = g.scalar if i % 2 == 0 else g.sync
+        q.wait_ge(S.vd, idx[(R, b - 1)] + 1)
+        q.dma_start(T.y[:, B * a:B * b], H[R][:, B * a:B * b]).then_inc(S.st, 16)
+
+    if sent:
+        g.wait_ge(S.sent, sent)
+    g.wait_ge(S.st, 16 * len(STORES))

@@ -4,9 +4,10 @@ from concourse.mybir import AluOpType
 N, NB, B = 4, 12, 32
 XO = 256
 W = XO + NB * B
-J = [6, 4, 4, 6]
+J = [4, 4, 4, 6]
 STORES = [(0, 5), (5, 9), (9, 11), (11, 12)]
 NBANK = 8
+JIT = 2
 
 SCRATCH = {
     "isrc": ("sbuf", [128, 129], "bfloat16"),
@@ -29,19 +30,26 @@ def _count(m):
     return bin(m).count("1")
 
 
-def _plan(q, cores, topo):
+def _masks(q, cores, topo):
     src = cores[q]
     dests = list(range(N - 1, q, -1))
     narrow = topo.mask(src, cores[dests[0]])
     for d in dests:
         narrow &= topo.mask(src, cores[d])
-    rounds = []
+    out = []
     for d in dests:
         m = topo.mask(src, cores[d])
         if topo.chip(src) != topo.chip(cores[d]):
             m = narrow
         else:
             m = (m & ~narrow) or m
+        out.append((d, m))
+    return out
+
+
+def _group(dm):
+    rounds = []
+    for d, m in dm:
         for rd in rounds:
             if all((m & mm) == 0 for _, mm in rd):
                 rd.append((d, m))
@@ -88,31 +96,35 @@ def rank_program(g, core, T, topo):
     sent = 0
     if R < N - 1:
         lo = 0 if R > 0 else 128
-        pieces = [(lo, split), (split, W)]
-        rounds = _plan(R, cores, topo)
-        for p, (a, b) in enumerate(pieces):
-            g.wait_ge(S.ld1 if p == 0 else S.ld2, LD1 if p == 0 else 16)
-            for rd in rounds:
-                trs = []
-                for d, m in rd:
-                    assert topo.may_write(core, cores[d])
-                    rid, pid, _ = topo.addr(cores[d])
-                    trs.append(RemoteDMATransfer(dst_ids=[DstId(rid=rid, pnc=pid)], dma_engine_mask=m,
-                                                 remote_sem=S["a%d_%d" % (R, p)], src=own[:, a:b], dst=own[:, a:b]))
-                    sent += _count(m)
-                g.remote_dma_fused(trs, local_sem=S.sent)
+        dm = _masks(R, cores, topo)
+        calls = [(0, lo, split, rd) for rd in [dm[:1]] + _group(dm[1:])]
+        calls += [(1, split, W, rd) for rd in _group(dm)]
+        g.wait_ge(S.ld1, LD1)
+        waited2 = False
+        for p, a, b, rd in calls:
+            if p == 1 and not waited2:
+                g.wait_ge(S.ld2, 16)
+                waited2 = True
+            trs = []
+            for d, m in rd:
+                assert topo.may_write(core, cores[d])
+                rid, pid, _ = topo.addr(cores[d])
+                trs.append(RemoteDMATransfer(dst_ids=[DstId(rid=rid, pnc=pid)], dma_engine_mask=m,
+                                             remote_sem=S["a%d_%d" % (R, p)], src=own[:, a:b], dst=own[:, a:b]))
+                sent += _count(m)
+            g.remote_dma_fused(trs, local_sem=S.sent)
 
     arrive = {}
     for q in range(R):
-        for rd in _plan(q, cores, topo):
-            for d, m in rd:
-                if d == R:
-                    arrive[q] = _count(m)
+        for d, m in _masks(q, cores, topo):
+            if d == R:
+                arrive[q] = _count(m)
 
-    order = [(r, s - r) for s in range(NB + R) for r in range(R + 1) if 0 <= s - r < NB]
+    steps = [[(r, s - r) for r in range(R + 1) if 0 <= s - r < NB] for s in range(NB + R)]
+    order = [nd for stp in steps for nd in stp]
     idx = {nd: i for i, nd in enumerate(order)}
     mn = [nd for nd in order if nd != (0, 0)]
-    ahead = max(2, R + 1)
+    kof = {nd: k for k, nd in enumerate(mn)}
     seen = set()
     tw = [0]
 
@@ -130,8 +142,9 @@ def rank_program(g, core, T, topo):
             te.wait_ge(S.vd, n)
             tw[0] = n
 
-    def preload(k):
-        r, c = mn[k]
+    def preload(nd):
+        r, c = nd
+        k = kof[nd]
         here(te, "t", r, 0)
         if c >= J[r]:
             here(te, "t", r, 1)
@@ -139,29 +152,35 @@ def rank_program(g, core, T, topo):
             done(idx[mn[k - NBANK]] + 1)
         te.matmul(ps[k % NBANK][:, 0:B], ident, inb[r][:, XO + B * c:XO + B * c + B], True, False)
 
-    te.wait_ge(S.idn, 16)
-    here(ve, "v", 0, 0)
-    ve.tensor_tensor(H[0][:, 0:B], inb[0][:, XO:XO + B], T.zb[:, :], AluOpType.max).then_inc(S.vd, 1)
-    for k in range(min(ahead, len(mn))):
-        preload(k)
-    for k, (r, c) in enumerate(mn):
-        if k + ahead < len(mn):
-            preload(k + ahead)
+    def block(nd):
+        r, c = nd
+        k = kof[nd]
         acc = ps[k % NBANK][:, 0:B]
         mms = []
-        need = 0
         if r > 0:
-            mms.append((inb[r][:, 0:128], H[r - 1][:, B * c:B * c + B]))
-            need = max(need, idx[(r - 1, c)] + 1)
+            mms.append((inb[r][:, 0:128], H[r - 1][:, B * c:B * c + B], idx[(r - 1, c)] + 1))
         if c > 0:
-            mms.append((inb[r][:, 128:256], H[r][:, B * (c - 1):B * c]))
-            need = max(need, idx[(r, c - 1)] + 1)
-        done(need)
-        for i, (w, h) in enumerate(mms):
+            mms.append((inb[r][:, 128:256], H[r][:, B * (c - 1):B * c], idx[(r, c - 1)] + 1))
+        for i, (w, h, need) in enumerate(mms):
+            done(need)
             ins = te.matmul(acc, w, h, False, i == len(mms) - 1)
         ins.then_inc(S.mm, 1)
         ve.wait_ge(S.mm, k + 1)
         ve.tensor_tensor(H[r][:, B * c:B * c + B], acc, T.zeros[:, :], AluOpType.max).then_inc(S.vd, 1)
+
+    te.wait_ge(S.idn, 16)
+    here(ve, "v", 0, 0)
+    ve.tensor_tensor(H[0][:, 0:B], inb[0][:, XO:XO + B], T.zb[:, :], AluOpType.max).then_inc(S.vd, 1)
+    for s, stp in enumerate(steps):
+        for nd in stp:
+            if nd == (0, 0):
+                continue
+            if s <= JIT:
+                preload(nd)
+            block(nd)
+        if s >= JIT and s + 1 < len(steps):
+            for nd in reversed(steps[s + 1]):
+                preload(nd)
 
     for i, (a, b) in enumerate(STORES):
         q = g.scalar if i % 2 == 0 else g.sync

from concourse.bass import DstId, RemoteDMATransfer
from concourse.mybir import AluOpType

N, NB, B = 4, 12, 32
XO = 256
W = XO + NB * B
J = [4, 4, 4, 6]
STORES = [(0, 5), (5, 9), (9, 11), (11, 12)]
NBANK = 8
JIT = 2

SCRATCH = {
    "isrc": ("sbuf", [128, 129], "bfloat16"),
    "idd": ("dram", [1, 128 * 129], "bfloat16"),
    "ident": ("sbuf", [128, 128], "bfloat16"),
    "zeros": ("sbuf", [128, B], "float32"),
    "zb": ("sbuf", [128, B], "bfloat16"),
}
for _q in range(N):
    SCRATCH["inb%d" % _q] = ("sbuf", [128, W], "bfloat16")
    SCRATCH["h%d" % _q] = ("sbuf", [128, NB * B], "bfloat16")
for _b in range(NBANK):
    SCRATCH["ps%d" % _b] = ("psum", [128, 512], "float32")

SEMAPHORES = ["ld1", "ld2", "ms", "idw", "idn", "mm", "vd", "st", "sent"] + [
    "a%d_%d" % (q, p) for q in range(N - 1) for p in range(2)]


def _count(m):
    return bin(m).count("1")


def _masks(q, cores, topo):
    src = cores[q]
    dests = list(range(N - 1, q, -1))
    narrow = topo.mask(src, cores[dests[0]])
    for d in dests:
        narrow &= topo.mask(src, cores[d])
    out = []
    for d in dests:
        m = topo.mask(src, cores[d])
        if topo.chip(src) != topo.chip(cores[d]):
            m = narrow
        else:
            m = (m & ~narrow) or m
        out.append((d, m))
    return out


def _group(dm):
    rounds = []
    for d, m in dm:
        for rd in rounds:
            if all((m & mm) == 0 for _, mm in rd):
                rd.append((d, m))
                break
        else:
            rounds.append([(d, m)])
    return rounds


def rank_program(g, core, T, topo):
    R = T.rank_of(core)
    if R is None:
        return
    S = T.sem
    cores = list(T.cores)
    inb = [T["inb%d" % q] for q in range(N)]
    H = [T["h%d" % q] for q in range(N)]
    ps = [T["ps%d" % b] for b in range(NBANK)]
    te, ve = g.tensor, g.vector
    own = inb[R]
    split = XO + B * J[R]

    g.sync.dma_start(own[:, 128:256], T.wh[:, :]).then_inc(S.ld1, 16)
    if R > 0:
        g.scalar.dma_start(own[:, 0:128], T.wv[:, :]).then_inc(S.ld1, 16)
        g.sync.dma_start(own[:, XO:split], T.x[:, 0:B * J[R]]).then_inc(S.ld1, 16)
        LD1 = 48
    else:
        g.scalar.dma_start(own[:, XO:split], T.x[:, 0:B * J[R]]).then_inc(S.ld1, 16)
        LD1 = 32
    g.sync.dma_start(own[:, split:W], T.x[:, B * J[R]:NB * B]).then_inc(S.ld2, 16)

    ve.memset(T.isrc[:, 0:1], 1.0).then_inc(S.ms, 1)
    ve.memset(T.isrc[:, 1:129], 0.0).then_inc(S.ms, 1)
    ve.memset(T.zeros[:, :], 0.0).then_inc(S.ms, 1)
    ve.memset(T.zb[:, :], 0.0).then_inc(S.ms, 1)
    ve.wait_ge(S.ms, 4)
    g.scalar.wait_ge(S.ms, 4)
    g.scalar.dma_start(T.idd[0, :], T.isrc[:, :]).then_inc(S.idw, 16)
    g.scalar.wait_ge(S.idw, 16)
    g.scalar.dma_start(T.ident[:, :], T.idd[0, 0:128 * 128]).then_inc(S.idn, 16)
    ident = T.ident[:, :]

    sent = 0
    if R < N - 1:
        lo = 0 if R > 0 else 128
        dm = _masks(R, cores, topo)
        calls = [(0, lo, split, rd) for rd in [dm[:1]] + _group(dm[1:])]
        calls += [(1, split, W, rd) for rd in _group(dm)]
        g.wait_ge(S.ld1, LD1)
        waited2 = False
        for p, a, b, rd in calls:
            if p == 1 and not waited2:
                g.wait_ge(S.ld2, 16)
                waited2 = True
            trs = []
            for d, m in rd:
                assert topo.may_write(core, cores[d])
                rid, pid, _ = topo.addr(cores[d])
                trs.append(RemoteDMATransfer(dst_ids=[DstId(rid=rid, pnc=pid)], dma_engine_mask=m,
                                             remote_sem=S["a%d_%d" % (R, p)], src=own[:, a:b], dst=own[:, a:b]))
                sent += _count(m)
            g.remote_dma_fused(trs, local_sem=S.sent)

    arrive = {}
    for q in range(R):
        for d, m in _masks(q, cores, topo):
            if d == R:
                arrive[q] = _count(m)

    steps = [[(r, s - r) for r in range(R + 1) if 0 <= s - r < NB] for s in range(NB + R)]
    order = [nd for stp in steps for nd in stp]
    idx = {nd: i for i, nd in enumerate(order)}
    mn = [nd for nd in order if nd != (0, 0)]
    kof = {nd: k for k, nd in enumerate(mn)}
    seen = set()
    tw = [0]

    def here(queue, tag, r, half):
        if (tag, r, half) in seen:
            return
        seen.add((tag, r, half))
        if r == R:
            queue.wait_ge(S.ld1 if half == 0 else S.ld2, LD1 if half == 0 else 16)
        else:
            queue.wait_ge(S["a%d_%d" % (r, half)], arrive[r])

    def done(n):
        if n > tw[0]:
            te.wait_ge(S.vd, n)
            tw[0] = n

    def preload(nd):
        r, c = nd
        k = kof[nd]
        here(te, "t", r, 0)
        if c >= J[r]:
            here(te, "t", r, 1)
        if k >= NBANK:
            done(idx[mn[k - NBANK]] + 1)
        te.matmul(ps[k % NBANK][:, 0:B], ident, inb[r][:, XO + B * c:XO + B * c + B], True, False)

    def block(nd):
        r, c = nd
        k = kof[nd]
        acc = ps[k % NBANK][:, 0:B]
        mms = []
        if r > 0:
            mms.append((inb[r][:, 0:128], H[r - 1][:, B * c:B * c + B], idx[(r - 1, c)] + 1))
        if c > 0:
            mms.append((inb[r][:, 128:256], H[r][:, B * (c - 1):B * c], idx[(r, c - 1)] + 1))
        for i, (w, h, need) in enumerate(mms):
            done(need)
            ins = te.matmul(acc, w, h, False, i == len(mms) - 1)
        ins.then_inc(S.mm, 1)
        ve.wait_ge(S.mm, k + 1)
        ve.tensor_tensor(H[r][:, B * c:B * c + B], acc, T.zeros[:, :], AluOpType.max).then_inc(S.vd, 1)

    te.wait_ge(S.idn, 16)
    here(ve, "v", 0, 0)
    ve.tensor_tensor(H[0][:, 0:B], inb[0][:, XO:XO + B], T.zb[:, :], AluOpType.max).then_inc(S.vd, 1)
    for s, stp in enumerate(steps):
        for nd in stp:
            if nd == (0, 0):
                continue
            if s <= JIT:
                preload(nd)
            block(nd)
        if s >= JIT and s + 1 < len(steps):
            for nd in reversed(steps[s + 1]):
                preload(nd)

    for i, (a, b) in enumerate(STORES):
        q = g.scalar if i % 2 == 0 else g.sync
        q.wait_ge(S.vd, idx[(R, b - 1)] + 1)
        q.dma_start(T.y[:, B * a:B * b], H[R][:, B * a:B * b]).then_inc(S.st, 16)

    if sent:
        g.wait_ge(S.sent, sent)
    g.wait_ge(S.st, 16 * len(STORES))
